import numpy as np, ml_dtypes
CORES = [96,97,98,99,224,225,226,227,352,353,354,355,480,481,482,483]
N = 16
def setup_inputs(rng):
    return {"x": rng.standard_normal((N, 128, 8), dtype=np.float32).astype(ml_dtypes.bfloat16)}
def reference(x):
    s = x.max(axis=0)
    return {"y": np.broadcast_to(s, (N,) + s.shape)}

from concourse.bass import DstId, RemoteDMATransfer

COLS = 8
HELPER = 4
MAX = 2

SCRATCH = {
    "land": ("dram", [9, 128, COLS], "bfloat16"),
}
SEMAPHORES = ["ld", "st", "raw", "part", "res", "sent"]


def _dst(topo, d, core):
    rid, pid = topo.addr(d, core)
    return DstId(rid=rid, pnc=pid)


def rank_program(g, core, T, topo):
    chip0 = core - core % 8
    if T.rank_of(chip0) is None:
        return
    h = topo.host(core)
    k = core % 8
    land = T.land
    helper = lambda host: host * 128 + chip0 % 128 + HELPER

    if T.rank_of(core) is not None:
        g.sync.dma_start(land[0], T.x[:]).then_inc(T.sem.ld, 16)
        g.wait_ge(T.sem.ld, 16)
        g.remote_dma_fused([
            RemoteDMATransfer(dst_ids=[_dst(topo, helper(h ^ 1), core)], dma_engine_mask=0x000F,
                              remote_sem=T.sem.raw, src=land[0], dst=land[4 + k]),
            RemoteDMATransfer(dst_ids=[_dst(topo, helper(h), core)], dma_engine_mask=0x00F0,
                              remote_sem=T.sem.raw, src=land[0], dst=land[k]),
        ], local_sem=T.sem.sent)
        g.sync.wait_ge(T.sem.res, 4)
        g.sync.dma_start(T.y[:], land[8]).then_inc(T.sem.st, 16)
        g.sync.wait_ge(T.sem.st, 16)
        g.wait_ge(T.sem.sent, 8)
        return

    if k != HELPER:
        return

    g.wait_ge(T.sem.raw, 8 * 4)
    g.remote_dma_fused([
        RemoteDMATransfer(dst_ids=[_dst(topo, helper(3 - h), core)], dma_engine_mask=0x000F,
                          remote_sem=T.sem.part, srcs=[land[i] for i in range(8)], dsts=[land[8]], alu_op=MAX),
    ], local_sem=T.sem.sent)
    g.wait_ge(T.sem.part, 4)
    g.remote_dma_fused([
        RemoteDMATransfer(dst_ids=[_dst(topo, chip0 + j, core)], dma_engine_mask=0xF << (4 * j),
                          remote_sem=T.sem.res, srcs=[land[i] for i in range(9)], dsts=[land[8]], alu_op=MAX)
        for j in range(4)
    ], local_sem=T.sem.sent)
    g.wait_ge(T.sem.sent, 4 + 16)
